import numpy as np
import ml_dtypes


def mxq(x, axis, fmt="e4m3"):
    dtype, down = {"e4m3": (ml_dtypes.float8_e4m3fn, 7), "e5m2": (ml_dtypes.float8_e5m2, 14)}[fmt]
    v = np.moveaxis(np.asarray(x, np.float32).astype(ml_dtypes.bfloat16).astype(np.float64), axis, -1)
    blocks = v.reshape(v.shape[:-1] + (-1, 32))
    amax = np.abs(blocks).max(-1, keepdims=True)
    byte = np.maximum(np.where(amax > 0, np.frexp(amax)[1] - 1 + 127, 0) - down, 1)
    scale = np.exp2(byte - 127.0)
    codes = (blocks / scale).astype(np.float32).astype(dtype).astype(np.float64)
    return np.moveaxis((codes * scale).reshape(v.shape), -1, axis)


WIDE = False


def mx_kscale(k):
    if not WIDE:
        return np.ones(k)
    levels = np.array([10, -10, 5, -5, 0])
    if k % 512:
        return np.exp2(np.random.permutation(np.resize(levels, k // 32))).repeat(32)
    a = np.empty((k // 512, 16))
    for p in range(k // 512):
        a[p, :8] = np.random.permutation(np.resize(levels, 8))
        for g in range(8):
            far = levels[np.abs(levels - a[p, g]) >= 10]
            a[p, g + 8] = far[np.random.randint(len(far))]
    return np.exp2(a.ravel()).repeat(32)


def f64(x):
    return np.asarray(x).astype(np.float64)


def striped(idx):
    return np.tile(idx.reshape(-1, 16).T, (8, 1)).astype(np.uint16)


def unstriped(offs):
    return offs[:16].T.reshape(-1).astype(np.int64)


E2M1 = np.array([0.0, 0.5, 1.0, 1.5, 2.0, 3.0, 4.0, 6.0, -0.0, -0.5, -1.0, -1.5, -2.0, -3.0, -4.0, -6.0])


def pack_weight(w, fmt):
    k, n = w.shape
    w = f64(np.asarray(w, np.float32).astype(ml_dtypes.bfloat16)).reshape(k // 32, 32, n)
    amax = np.abs(w).max(1)
    if fmt == "e4m3":
        byte = np.frexp(amax)[1] - 1 + 127 - 7
    else:
        mant, ex = np.frexp(amax / 6.0)
        byte = np.where(mant > 0.5, ex, ex - 1) + 127
    byte = np.clip(np.where(amax > 0, byte, 1), 1, 254)
    scaled = (w * np.exp2(127.0 - byte)[:, None, :]).reshape(k, n).astype(np.float32)
    by_word = np.ascontiguousarray(scaled.reshape(k // 512, 128, 4, n).transpose(0, 1, 3, 2))
    if fmt == "e4m3":
        words = by_word.astype(ml_dtypes.float8_e4m3fn).view(np.uint8)
    else:
        c = by_word.astype(ml_dtypes.float4_e2m1fn).view(np.uint8) & 0xF
        words = (c[..., 0::2] | (c[..., 1::2] << 4)).reshape(k // 512, 128, 2 * n)
    return np.ascontiguousarray(words), np.ascontiguousarray(byte.astype(np.uint8).reshape(k // 512, 16, n))


def unpack_weight(words, scales, fmt):
    g, _, n = scales.shape
    words = np.ascontiguousarray(words).reshape(g, 128, n, -1)
    if fmt == "e4m3":
        vals = words.view(ml_dtypes.float8_e4m3fn).astype(np.float64)
    else:
        nib = np.empty((g, 128, n, 4), np.uint8)
        nib[..., 0::2] = words & 0xF
        nib[..., 1::2] = words >> 4
        vals = E2M1[nib]
    vals = vals * np.repeat(np.exp2(scales.astype(np.float64) - 127.0), 8, axis=1)[..., None]
    return vals.transpose(0, 1, 3, 2).reshape(g * 512, n)


def gelu(v):
    return 0.5 * v * (1.0 + np.tanh(np.sqrt(2.0 / np.pi) * (v + 0.044715 * v**3)))


def striped8(idx):
    return np.concatenate([v.reshape(-1, 16).T for v in idx]).astype(np.uint16)


def unstriped8(offs):
    return np.stack([offs[16 * g:16 * g + 16].T.reshape(-1) for g in range(8)]).astype(np.int64)


def heads(h, wgt, idx8):
    r = np.arange(h.shape[0])
    return wgt[r // 4 % 128] * h[r[:, None], idx8[r % 512 // 64]]


def put_heads(h, wgs, idx8, t2):
    r = np.arange(h.shape[0])
    page = np.zeros((h.shape[0], t2))
    page[r[:, None], idx8[r % 512 // 64]] = wgs[r // 4 % 128] * h
    return page


K, T, H, S, P, N, T2 = 1536, 4096, 1024, 1024, 512, 512, 1024

def setup_inputs():
    n = np.random.standard_normal
    s = mx_kscale(K)[:, None]
    u = mx_kscale(H)[:, None]
    d = {}
    d["tab_words"], d["tab_scales"] = pack_weight(n((K, T)) * s, "e4m3")
    d["offs"] = striped(np.random.permutation(T)[:S])
    d["w1"] = (n((K, H)) / s / K**0.5).astype(np.float32)
    d["gain"] = np.exp(0.3 * n(H)).astype(np.float32)
    d["offs2"] = striped8(np.stack([np.random.permutation(S)[:P] for _ in range(8)]))
    d["wgt"] = np.repeat(np.random.uniform(0.5, 2.0, (8, P)), 16, axis=0).astype(np.float32)
    d["hum"] = (0.8 * n((H, P))).astype(np.float32)
    d["lift"] = (np.exp(0.3 * n(H)) * u[:, 0]).astype(np.float32)
    d["w4_words"], d["w4_scales"] = pack_weight(n((H, N)) / u / H**0.5, "e2m1")
    d["base"] = (0.6 * n(N)).astype(np.float32)
    d["offs3"] = striped8(np.stack([np.random.permutation(T2)[:P] for _ in range(8)]))
    d["wgo"] = np.repeat(np.random.uniform(0.5, 2.0, (8, P)), 16, axis=0).astype(np.float32)
    return d

def reference(tab_words, tab_scales, offs, w1, gain, offs2, wgt, hum, lift, w4_words, w4_scales, base, offs3, wgo):
    v = unpack_weight(tab_words, tab_scales, "e4m3")[:, unstriped(offs)]
    h = f64(gain)[:, None] * (mxq(f64(w1), 0, "e4m3").T @ v)
    x = heads(h, f64(wgt), unstriped8(offs2))
    z = f64(lift)[:, None] * np.tanh(x + f64(hum))
    w4 = unpack_weight(w4_words, w4_scales, "e2m1")
    y = (w4.T @ mxq(z, 0, "e4m3")) + f64(base)[:, None]
    return put_heads(y, f64(wgo), unstriped8(offs3), T2)

@@ -1,0 +1,301 @@
+from contextlib import ExitStack
+
+import concourse.mybir as mybir
+from concourse.masks import make_identity
+
+K, T, H, S, M, N, T2 = 1536, 4096, 1024, 1024, 512, 512, 1024
+FLOPS = 2 * K * H * S + 2 * H * N * M
+
+F32 = mybir.dt.float32
+BF16 = mybir.dt.bfloat16
+I32 = mybir.dt.int32
+U32 = mybir.dt.uint32
+U16 = mybir.dt.uint16
+U8 = mybir.dt.uint8
+FP8X4 = mybir.dt.float8_e4m3fn_x4
+FP4X4 = mybir.dt.float4_e2m1fn_x4
+ACT = mybir.ActivationFunctionType
+MULT = mybir.AluOpType.mult
+ADD = mybir.AluOpType.add
+
+P = 128
+MODE = "S"
+VECTOR_CASTS = ((0, 2, 0), (1, 2, 0), (1, 1, 0))
+SCALE_QUEUE = "sync"
+TAB_PIECES = (1, 1, 1)
+WARM = True
+
+
+def tile_list_leaf_grade_trays_kernel(
+    tc, tab_words, tab_scales, offs, w1, gain, offs2, wgt, hum, lift, w4_words, w4_scales, base, offs3, wgo, out
+):
+    nc = tc.nc
+    with ExitStack() as ctx:
+        lists = ctx.enter_context(tc.tile_pool(name="lists", bufs=1))
+        held = ctx.enter_context(tc.tile_pool(name="held", bufs=1))
+        ring = ctx.enter_context(tc.tile_pool(name="ring", bufs=4))
+        wide = ctx.enter_context(tc.tile_pool(name="wide", bufs=6))
+        psum = ctx.enter_context(tc.psum_pool(name="psum", bufs=1))
+        small_q = nc.gpsimd if SCALE_QUEUE == "gpsimd" else nc.sync
+
+        def bank(n, name):
+            return psum.tile([P, 512], F32, name=name, tag="bank%d" % n)
+
+        tab_s = held.tile([P, T], U8, name="tab_s")
+        nc.vector.memset(tab_s[:].bitcast(I32), 0)
+        w4s_raw = held.tile([P, 2, N], U8, name="w4s_raw")
+        nc.vector.memset(w4s_raw[:].bitcast(I32), 0)
+
+        tab_w = [held.tile([P, T], U32, name="tab_w%d" % a) for a in range(3)]
+        raw = {}
+
+        def load_tab(a):
+            words = tab_words[a].rearrange("p t i -> p (t i)").bitcast(I32)
+            step = T // TAB_PIECES[a]
+            for lo in range(0, T, step):
+                nc.sync.dma_start(out=tab_w[a][:, lo : lo + step].bitcast(I32), in_=words[:, lo : lo + step])
+
+        def load_w1(b, a):
+            raw[b, a] = wide.tile([P, 4, 512], F32, name="raw%d%d" % (b, a), tag="wide")
+            nc.sync.dma_start(
+                out=raw[b, a][:],
+                in_=w1[512 * a : 512 * (a + 1), 512 * b : 512 * (b + 1)].rearrange("(p j) c -> p j c", j=4),
+            )
+
+        list1 = lists.tile([P, S // 16], U16, name="list1")
+        list2 = lists.tile([P, M // 16], U16, name="list2")
+        list3 = lists.tile([P, M // 16], U16, name="list3")
+        gain_t = held.tile([P, 2, 4], F32, name="gain_t", tag="gain_then_x")
+        lift_t = held.tile([P, 2, 4], F32, name="lift_t")
+        base_t = held.tile([P, 4], F32, name="base_t")
+        w4_raw = held.tile([P, 2, 2 * N], U8, name="w4_raw")
+        wgt_t = held.tile([P, M], F32, name="wgt_t")
+        wgo_t = held.tile([P, M], F32, name="wgo_t")
+        hum_t = [held.tile([P, 4, M], F32, name="hum_t%d" % b) for b in range(2)]
+
+        load_tab(0)
+        nc.sync.dma_start(list1[:], offs)
+        nc.sync.dma_start(list2[:], offs2)
+        nc.sync.dma_start(list3[:], offs3)
+        nc.sync.dma_start(out=gain_t[:], in_=gain.rearrange("(b p i) -> p b i", b=2, i=4))
+        nc.sync.dma_start(out=lift_t[:], in_=lift.rearrange("(b p i) -> p b i", b=2, i=4))
+        load_w1(0, 0)
+        nc.sync.dma_start(out=w4_raw[:].bitcast(I32), in_=w4_words.rearrange("a p c -> p a c").bitcast(I32))
+        for q in range(4):
+            small_q.dma_start(
+                out=tab_s[32 * q : 32 * q + 12, :].bitcast(I32), in_=tab_scales[:, 4 * q : 4 * q + 4, :].bitcast(I32)
+            )
+        load_tab(1)
+        load_w1(0, 1)
+        for q in range(4):
+            nc.sync.dma_start(
+                out=w4s_raw[32 * q : 32 * q + 4, :, :].bitcast(I32),
+                in_=w4_scales[:, 4 * q : 4 * q + 4, :].rearrange("a r n -> r a n").bitcast(I32),
+            )
+        load_tab(2)
+        load_w1(0, 2)
+        nc.sync.dma_start(out=wgt_t[:], in_=wgt)
+        for a in range(3):
+            load_w1(1, a)
+        for b in range(2):
+            nc.sync.dma_start(out=hum_t[b][:], in_=hum[512 * b : 512 * (b + 1), :].rearrange("(p i) m -> p i m", i=4))
+        nc.sync.dma_start(out=base_t[:], in_=base.rearrange("(p i) -> p i", i=4))
+        nc.sync.dma_start(out=wgo_t[:], in_=wgo)
+
+        ident = held.tile([P, P], F32, name="ident")
+        make_identity(nc, ident[:])
+        if WARM:
+            warm = held.tile([P, 1], F32, name="warm")
+            nc.scalar.activation(out=warm[:], in_=ident[:, 0:1], func=ACT.Tanh)
+
+        pages = [held.tile([P, T2], F32, name="page%d" % i) for i in range(4)]
+        for i in range(4):
+            nc.vector.memset(pages[i][:], 0.0)
+
+        got_w = [held.tile([P, S], U32, name="got_w%d" % a, align_bytes=64) for a in range(3)]
+        got_s = held.tile([P, S], U8, name="got_s", align_bytes=64)
+
+        codes, scales = {}, {}
+
+        def quantize_w1(b, a):
+            grouped = []
+            for u in range(2):
+                g = ring.tile([P, 1024], BF16, name="grouped%d%d%d" % (b, a, u), tag="grouped", align_bytes=64)
+                dst = g[:].rearrange("p (t m j) -> p m j t", t=2, j=4)
+                src = raw[b, a][:].rearrange("p j (m t) -> p m j t", t=4)[:, :, :, 2 * u : 2 * u + 2]
+                if (b, a, u) in VECTOR_CASTS:
+                    nc.vector.tensor_copy(out=dst, in_=src)
+                else:
+                    nc.scalar.copy(out=dst, in_=src)
+                grouped.append(g)
+            for u in range(2):
+                codes[b, a, u] = held.tile([P, 256], U32, name="codes%d%d%d" % (b, a, u), align_bytes=64)
+                scales[b, a, u] = held.tile([P, 256], U8, name="scales%d%d%d" % (b, a, u), align_bytes=64)
+                nc.vector.quantize_mx(out=codes[b, a, u][:].bitcast(FP8X4), scales=scales[b, a, u][:], in_=grouped[u][:])
+
+        def stage1(acc, b, i, s, a):
+            cols = slice(128 * (i % 2), 128 * (i % 2) + 128)
+            nc.tensor.matmul_mx(
+                out=acc[:],
+                lhsT=codes[b, a, i // 2][:, cols].bitcast(FP8X4),
+                lhsT_scale=scales[b, a, i // 2][:, cols],
+                rhs=got_w[a][:, 512 * s : 512 * (s + 1)].bitcast(FP8X4),
+                rhs_scale=got_s[4 * a : P, 512 * s : 512 * (s + 1)],
+                start=(a == 0),
+                stop=(a == 2),
+            )
+
+        x = {}
+        h = {}
+
+        def empty_h(b, i, accs):
+            h[b, i] = ring.tile([P, S], F32, name="h%d%d" % (b, i), tag="h")
+            for s in range(2):
+                if (b, i, s) == (0, 0, 1):
+                    nc.vector.tensor_scalar(h[b, i][:, 512:1024], accs[s][:], gain_t[:, b, i : i + 1], None, MULT)
+                else:
+                    nc.scalar.activation(
+                        out=h[b, i][:, 512 * s : 512 * (s + 1)], in_=accs[s][:], func=ACT.Copy, scale=gain_t[:, b, i : i + 1]
+                    )
+
+        def x_at(b, i, lo, hi):
+            if b == 0:
+                return x[0][:, i, lo:hi]
+            return x[1, lo // 256][:, i, lo % 256 : lo % 256 + hi - lo]
+
+        def pick(b, i, lo, hi):
+            nc.vector.tensor_tensor(
+                x_at(b, i, lo, hi), h[b, i][:].indirect(list2[:, lo // 16 : hi // 16]), wgt_t[:, lo:hi], MULT
+            )
+
+        accs0 = [[bank(2 * i + s, "h0_%d%d" % (i, s)) for s in range(2)] for i in range(4)]
+        w4_p = held.tile([P, 2, 2 * N], U8, name="w4_p", align_bytes=64)
+        w4s_p = held.tile([P, 2, N], U8, name="w4s_p", align_bytes=64)
+        for a in range(3):
+            nc.vector.tensor_copy(got_w[a][:], tab_w[a][:].indirect(list1[:]))
+            if a == 0:
+                nc.vector.tensor_copy(got_s[:], tab_s[:].indirect(list1[:]))
+            quantize_w1(0, a)
+            for i in range(4):
+                for s in range(2):
+                    stage1(accs0[i][s], 0, i, s, a)
+            if a == 0:
+                nc.vector.tensor_copy(
+                    out=w4_p[:].rearrange("p a (i q e) -> p a q i e", i=4, e=2),
+                    in_=w4_raw[:].rearrange("p a (q i e) -> p a q i e", i=4, e=2),
+                )
+                nc.vector.tensor_copy(
+                    out=w4s_p[:].rearrange("p a (i q) -> p a q i", i=4),
+                    in_=w4s_raw[:].rearrange("p a (q i) -> p a q i", i=4),
+                )
+        x[0] = wide.tile([P, 4, M], F32, name="x0", tag="wide")
+        for i in range(4):
+            empty_h(0, i, accs0[i])
+            pick(0, i, 0, M)
+
+        x[1, 0] = wide.tile([P, 4, 256], F32, name="x10", tag="wide")
+        nb = 4 if MODE == "T" else 8
+        early = nb // 2
+        accs1 = [[bank((2 * i + s) % nb, "h1_%d%d" % (i, s)) for s in range(2)] for i in range(early)]
+        for a in range(3):
+            quantize_w1(1, a)
+            for i in range(early):
+                for s in range(2):
+                    stage1(accs1[i][s], 1, i, s, a)
+        for i in range(4):
+            if i >= early:
+                accs1.append([bank((2 * i + s) % nb, "h1_%d%d" % (i, s)) for s in range(2)])
+                for s in range(2):
+                    for a in range(3):
+                        stage1(accs1[i][s], 1, i, s, a)
+            empty_h(1, i, accs1[i])
+            pick(1, i, 0, 256)
+        x[1, 1] = held.tile([P, 4, 256], F32, name="x11", tag="gain_then_x")
+        for i in range(4):
+            pick(1, i, 256, 512)
+
+        zc, zs, ysb = {}, {}, {}
+
+        def make_z_T(b, c):
+            cols = slice(128 * c, 128 * (c + 1))
+            turned = bank((2 if b == 1 and c >= 2 else 4) + c % 2, "turned%d%d" % (b, c))
+            for i in range(4):
+                nc.tensor.matmul(
+                    turned[:, 128 * i : 128 * (i + 1)], hum_t[b][:, i, cols], ident[:],
+                    start=(i == 0), stop=False, is_transpose=True,
+                )
+            for i in range(4):
+                nc.tensor.matmul(
+                    turned[:, 128 * i : 128 * (i + 1)], x_at(b, i, 128 * c, 128 * (c + 1)), ident[:],
+                    start=False, stop=(i == 3), is_transpose=True,
+                )
+            bounded = ring.tile([P, 512], F32, name="bounded%d%d" % (b, c), tag="bounded")
+            nc.scalar.activation(out=bounded[:], in_=turned[:], func=ACT.Tanh)
+            back = bank(6 + c % 2, "back%d%d" % (b, c))
+            for i in range(4):
+                nc.tensor.transpose(back[:, 128 * i : 128 * (i + 1)], bounded[:, 128 * i : 128 * (i + 1)], ident[:])
+            zb = held.tile([P, 128, 4], BF16, name="zb%d%d" % (b, c), tag="zb%d" % c, align_bytes=64)
+            nc.vector.tensor_tensor(
+                zb[:], back[:].rearrange("p (i m) -> p m i", i=4), lift_t[:, b : b + 1, :].to_broadcast([P, 128, 4]), MULT
+            )
+            return zb
+
+        def make_z_S(b, c):
+            cols = slice(128 * c, 128 * (c + 1))
+            summed = ring.tile([P, 4, 128], F32, name="summed%d%d" % (b, c), tag="summed")
+            nc.vector.tensor_tensor(summed[:], x_at(b, slice(0, 4), 128 * c, 128 * (c + 1)), hum_t[b][:, :, cols], ADD)
+            bounded = ring.tile([P, 128, 4], F32, name="bounded%d%d" % (b, c), tag="bounded")
+            nc.scalar.activation(out=bounded[:], in_=summed[:].rearrange("p i m -> p m i"), func=ACT.Tanh)
+            zb = held.tile([P, 128, 4], BF16, name="zb%d%d" % (b, c), tag="zb%d" % c, align_bytes=64)
+            nc.vector.tensor_tensor(zb[:], bounded[:], lift_t[:, b : b + 1, :].to_broadcast([P, 128, 4]), MULT)
+            return zb
+
+        def make_z(b, pair):
+            made = [(c, (make_z_T if MODE == "T" else make_z_S)(b, c)) for c in pair]
+            for c, zb in made:
+                zc[b, c] = held.tile([P, 128], U32, name="zc%d%d" % (b, c), align_bytes=64)
+                zs[b, c] = held.tile([P, 128], U8, name="zs%d%d" % (b, c), align_bytes=64)
+                nc.vector.quantize_mx(
+                    out=zc[b, c][:].bitcast(FP8X4), scales=zs[b, c][:], in_=zb[:].rearrange("p m i -> p (m i)")
+                )
+
+        make_z(0, (0, 1))
+        make_z(0, (2, 3))
+        make_z(1, (0, 1))
+        ybs = {}
+        for hf in range(2):
+            yb = [bank(4 * hf + ip, "y%d%d" % (hf, ip)) for ip in range(2)]
+            for b in range(2):
+                for ip in range(2):
+                    parts = [(i, c) for i in (2 * ip, 2 * ip + 1) for c in (2 * hf, 2 * hf + 1)]
+                    for i, c in parts:
+                        at = 256 * (i % 2) + 128 * (c % 2)
+                        nc.tensor.matmul_mx(
+                            out=yb[ip][:, at : at + 128],
+                            lhsT=w4_p[:, b, 256 * i : 256 * (i + 1)].bitcast(FP4X4),
+                            lhsT_scale=w4s_p[:, b, 128 * i : 128 * (i + 1)],
+                            rhs=zc[b, c][:].bitcast(FP8X4),
+                            rhs_scale=zs[b, c][:],
+                            start=(b == 0 and (i, c) == parts[0]),
+                            stop=(b == 1 and (i, c) == parts[-1]),
+                        )
+            ybs[hf] = yb
+            if hf == 0:
+                make_z(1, (2, 3))
+            for i in range(4):
+                tag = "zb%d" % (i + 1) if (hf == 0 and i in (1, 2)) else "ysb%d%d" % (hf, i)
+                ysb[hf, i] = held.tile([P, 256], F32, name="ysb%d%d" % (hf, i), tag=tag, align_bytes=64)
+                nc.scalar.activation(
+                    out=ysb[hf, i][:], in_=yb[i // 2][:, 256 * (i % 2) : 256 * (i % 2) + 256],
+                    func=ACT.Identity, bias=base_t[:, i : i + 1],
+                )
+
+        rows = out.rearrange("(p i) t -> p i t", i=4)
+        for hf in range(2):
+            for i in range(4):
+                nc.vector.tensor_tensor(
+                    pages[i][:].indirect(list3[:, 16 * hf : 16 * hf + 16]),
+                    ysb[hf, i][:], wgo_t[:, 256 * hf : 256 * (hf + 1)], MULT,
+                )
+                if hf == 1:
+                    nc.sync.dma_start(out=rows[:, i, :], in_=pages[i][:])

@@ -19,11 +19,8 @@ MULT = mybir.AluOpType.mult
 ADD = mybir.AluOpType.add
 
 P = 128
-MODE = "S"
-VECTOR_CASTS = ((0, 2, 0), (1, 2, 0), (1, 1, 0))
-SCALE_QUEUE = "sync"
-TAB_PIECES = (1, 1, 1)
-WARM = True
+VECTOR_CASTS = ((0, 2, 0),)
+SCALE_QUEUE = "gpsimd"
 
 
 def tile_list_leaf_grade_trays_kernel(
@@ -34,33 +31,49 @@ def tile_list_leaf_grade_trays_kernel(
         lists = ctx.enter_context(tc.tile_pool(name="lists", bufs=1))
         held = ctx.enter_context(tc.tile_pool(name="held", bufs=1))
         ring = ctx.enter_context(tc.tile_pool(name="ring", bufs=4))
+        pair = ctx.enter_context(tc.tile_pool(name="pair", bufs=2))
         wide = ctx.enter_context(tc.tile_pool(name="wide", bufs=6))
         psum = ctx.enter_context(tc.psum_pool(name="psum", bufs=1))
-        small_q = nc.gpsimd if SCALE_QUEUE == "gpsimd" else nc.sync
 
         def bank(n, name):
             return psum.tile([P, 512], F32, name=name, tag="bank%d" % n)
 
-        tab_s = held.tile([P, T], U8, name="tab_s")
+        tab_s = held.tile([P, T], U8, name="tab_s", tag="page1")
         nc.vector.memset(tab_s[:].bitcast(I32), 0)
         w4s_raw = held.tile([P, 2, N], U8, name="w4s_raw")
         nc.vector.memset(w4s_raw[:].bitcast(I32), 0)
 
-        tab_w = [held.tile([P, T], U32, name="tab_w%d" % a) for a in range(3)]
+        tab_w = [held.tile([P, T], U32, name="tab_w%d" % a, tag=("page0", "page2", "tab_w2")[a]) for a in range(3)]
         raw = {}
 
-        def load_tab(a):
+        def load_tab(a, pieces=1):
             words = tab_words[a].rearrange("p t i -> p (t i)").bitcast(I32)
-            step = T // TAB_PIECES[a]
-            for lo in range(0, T, step):
-                nc.sync.dma_start(out=tab_w[a][:, lo : lo + step].bitcast(I32), in_=words[:, lo : lo + step])
+            for lo in range(0, T, T // pieces):
+                hi = lo + T // pieces
+                nc.sync.dma_start(out=tab_w[a][:, lo:hi].bitcast(I32), in_=words[:, lo:hi])
 
-        def load_w1(b, a):
+        def load_w1(b, a, pieces=1):
             raw[b, a] = wide.tile([P, 4, 512], F32, name="raw%d%d" % (b, a), tag="wide")
-            nc.sync.dma_start(
-                out=raw[b, a][:],
-                in_=w1[512 * a : 512 * (a + 1), 512 * b : 512 * (b + 1)].rearrange("(p j) c -> p j c", j=4),
-            )
+            rows = w1[512 * a : 512 * (a + 1), 512 * b : 512 * (b + 1)].rearrange("(p j) c -> p j c", j=4)
+            for lo in range(0, 4, 4 // pieces):
+                hi = lo + 4 // pieces
+                nc.sync.dma_start(out=raw[b, a][:, lo:hi, :], in_=rows[:, lo:hi, :])
+
+        def load_tab_scales(queue):
+            for q in range(4):
+                queue.dma_start(
+                    out=tab_s[32 * q : 32 * q + 12, :].bitcast(I32), in_=tab_scales[:, 4 * q : 4 * q + 4, :].bitcast(I32)
+                )
+
+        def load_w4_scales(queue):
+            for q in range(4):
+                queue.dma_start(
+                    out=w4s_raw[32 * q : 32 * q + 4, :, :].bitcast(I32),
+                    in_=w4_scales[:, 4 * q : 4 * q + 4, :].rearrange("a r n -> r a n").bitcast(I32),
+                )
+
+        def load_hum(b):
+            nc.sync.dma_start(out=hum_t[b][:], in_=hum[512 * b : 512 * (b + 1), :].rearrange("(p i) m -> p i m", i=4))
 
         list1 = lists.tile([P, S // 16], U16, name="list1")
         list2 = lists.tile([P, M // 16], U16, name="list2")
@@ -68,49 +81,48 @@ def tile_list_leaf_grade_trays_kernel(
         gain_t = held.tile([P, 2, 4], F32, name="gain_t", tag="gain_then_x")
         lift_t = held.tile([P, 2, 4], F32, name="lift_t")
         base_t = held.tile([P, 4], F32, name="base_t")
-        w4_raw = held.tile([P, 2, 2 * N], U8, name="w4_raw")
+        w4_raw = held.tile([P, 2, 2 * N], U8, name="w4_raw", tag="page3")
         wgt_t = held.tile([P, M], F32, name="wgt_t")
         wgo_t = held.tile([P, M], F32, name="wgo_t")
         hum_t = [held.tile([P, 4, M], F32, name="hum_t%d" % b) for b in range(2)]
 
-        load_tab(0)
+        def load_small(which):
+            if which == "gain":
+                nc.sync.dma_start(out=gain_t[:], in_=gain.rearrange("(b p i) -> p b i", b=2, i=4))
+            if which == "lift":
+                nc.sync.dma_start(out=lift_t[:], in_=lift.rearrange("(b p i) -> p b i", b=2, i=4))
+            if which == "list2":
+                nc.sync.dma_start(list2[:], offs2)
+            if which == "list3":
+                nc.sync.dma_start(list3[:], offs3)
+
+        pieces = 4 if SCALE_QUEUE == "sync" else 1
+        load_tab(0, pieces)
         nc.sync.dma_start(list1[:], offs)
-        nc.sync.dma_start(list2[:], offs2)
-        nc.sync.dma_start(list3[:], offs3)
-        nc.sync.dma_start(out=gain_t[:], in_=gain.rearrange("(b p i) -> p b i", b=2, i=4))
-        nc.sync.dma_start(out=lift_t[:], in_=lift.rearrange("(b p i) -> p b i", b=2, i=4))
-        load_w1(0, 0)
+        load_w1(0, 0, 2 if SCALE_QUEUE == "sync" else 1)
         nc.sync.dma_start(out=w4_raw[:].bitcast(I32), in_=w4_words.rearrange("a p c -> p a c").bitcast(I32))
-        for q in range(4):
-            small_q.dma_start(
-                out=tab_s[32 * q : 32 * q + 12, :].bitcast(I32), in_=tab_scales[:, 4 * q : 4 * q + 4, :].bitcast(I32)
-            )
+        load_tab_scales(nc.sync if SCALE_QUEUE == "sync" else nc.gpsimd)
         load_tab(1)
         load_w1(0, 1)
-        for q in range(4):
-            nc.sync.dma_start(
-                out=w4s_raw[32 * q : 32 * q + 4, :, :].bitcast(I32),
-                in_=w4_scales[:, 4 * q : 4 * q + 4, :].rearrange("a r n -> r a n").bitcast(I32),
-            )
+        load_w4_scales(nc.sync)
         load_tab(2)
         load_w1(0, 2)
+        load_small("gain")
+        load_small("list2")
         nc.sync.dma_start(out=wgt_t[:], in_=wgt)
-        for a in range(3):
-            load_w1(1, a)
-        for b in range(2):
-            nc.sync.dma_start(out=hum_t[b][:], in_=hum[512 * b : 512 * (b + 1), :].rearrange("(p i) m -> p i m", i=4))
+        load_w1(1, 0)
+        load_w1(1, 1)
+        load_hum(0)
+        load_w1(1, 2)
+        load_small("lift")
+        load_hum(1)
+        load_small("list3")
         nc.sync.dma_start(out=base_t[:], in_=base.rearrange("(p i) -> p i", i=4))
         nc.sync.dma_start(out=wgo_t[:], in_=wgo)
 
         ident = held.tile([P, P], F32, name="ident")
         make_identity(nc, ident[:])
-        if WARM:
-            warm = held.tile([P, 1], F32, name="warm")
-            nc.scalar.activation(out=warm[:], in_=ident[:, 0:1], func=ACT.Tanh)
 
-        pages = [held.tile([P, T2], F32, name="page%d" % i) for i in range(4)]
-        for i in range(4):
-            nc.vector.memset(pages[i][:], 0.0)
 
         got_w = [held.tile([P, S], U32, name="got_w%d" % a, align_bytes=64) for a in range(3)]
         got_s = held.tile([P, S], U8, name="got_s", align_bytes=64)
@@ -118,27 +130,31 @@ def tile_list_leaf_grade_trays_kernel(
         codes, scales = {}, {}
 
         def quantize_w1(b, a):
+            parts = 2 if a == 2 else 1
+            wt = 4 // parts
             grouped = []
-            for u in range(2):
-                g = ring.tile([P, 1024], BF16, name="grouped%d%d%d" % (b, a, u), tag="grouped", align_bytes=64)
-                dst = g[:].rearrange("p (t m j) -> p m j t", t=2, j=4)
-                src = raw[b, a][:].rearrange("p j (m t) -> p m j t", t=4)[:, :, :, 2 * u : 2 * u + 2]
+            for u in range(parts):
+                g = ring.tile([P, 512 * wt], BF16, name="grouped%d%d%d" % (b, a, u), tag="grouped", align_bytes=64)
+                dst = g[:].rearrange("p (t m j) -> p m j t", t=wt, j=4)
+                src = raw[b, a][:].rearrange("p j (m t) -> p m j t", t=4)[:, :, :, wt * u : wt * (u + 1)]
                 if (b, a, u) in VECTOR_CASTS:
                     nc.vector.tensor_copy(out=dst, in_=src)
                 else:
-                    nc.scalar.copy(out=dst, in_=src)
+                    nc.scalar.activation(out=dst, in_=src, func=ACT.Copy)
                 grouped.append(g)
-            for u in range(2):
-                codes[b, a, u] = held.tile([P, 256], U32, name="codes%d%d%d" % (b, a, u), align_bytes=64)
-                scales[b, a, u] = held.tile([P, 256], U8, name="scales%d%d%d" % (b, a, u), align_bytes=64)
-                nc.vector.quantize_mx(out=codes[b, a, u][:].bitcast(FP8X4), scales=scales[b, a, u][:], in_=grouped[u][:])
+            for u in range(parts):
+                words = held.tile([P, 128 * wt], U32, name="codes%d%d%d" % (b, a, u), align_bytes=64)
+                plane = held.tile([P, 128 * wt], U8, name="scales%d%d%d" % (b, a, u), align_bytes=64)
+                nc.vector.quantize_mx(out=words[:].bitcast(FP8X4), scales=plane[:], in_=grouped[u][:])
+                for t in range(wt):
+                    codes[b, a, wt * u + t] = words[:, 128 * t : 128 * (t + 1)]
+                    scales[b, a, wt * u + t] = plane[:, 128 * t : 128 * (t + 1)]
 
         def stage1(acc, b, i, s, a):
-            cols = slice(128 * (i % 2), 128 * (i % 2) + 128)
             nc.tensor.matmul_mx(
                 out=acc[:],
-                lhsT=codes[b, a, i // 2][:, cols].bitcast(FP8X4),
-                lhsT_scale=scales[b, a, i // 2][:, cols],
+                lhsT=codes[b, a, i].bitcast(FP8X4),
+                lhsT_scale=scales[b, a, i],
                 rhs=got_w[a][:, 512 * s : 512 * (s + 1)].bitcast(FP8X4),
                 rhs_scale=got_s[4 * a : P, 512 * s : 512 * (s + 1)],
                 start=(a == 0),
@@ -168,103 +184,107 @@ def tile_list_leaf_grade_trays_kernel(
                 x_at(b, i, lo, hi), h[b, i][:].indirect(list2[:, lo // 16 : hi // 16]), wgt_t[:, lo:hi], MULT
             )
 
-        accs0 = [[bank(2 * i + s, "h0_%d%d" % (i, s)) for s in range(2)] for i in range(4)]
         w4_p = held.tile([P, 2, 2 * N], U8, name="w4_p", align_bytes=64)
         w4s_p = held.tile([P, 2, N], U8, name="w4s_p", align_bytes=64)
-        for a in range(3):
-            nc.vector.tensor_copy(got_w[a][:], tab_w[a][:].indirect(list1[:]))
-            if a == 0:
-                nc.vector.tensor_copy(got_s[:], tab_s[:].indirect(list1[:]))
-            quantize_w1(0, a)
+        for b in range(2):
+            accs = [[bank(2 * i + s, "h%d_%d%d" % (b, i, s)) for s in range(2)] for i in range(4)]
+            for a in range(3):
+                if b == 0:
+                    nc.vector.tensor_copy(got_w[a][:], tab_w[a][:].indirect(list1[:]))
+                    if a == 0:
+                        nc.vector.tensor_copy(got_s[:], tab_s[:].indirect(list1[:]))
+                quantize_w1(b, a)
+                for i in range(4):
+                    for s in range(2):
+                        stage1(accs[i][s], b, i, s, a)
+                if (b, a) == (0, 0):
+                    nc.vector.tensor_copy(
+                        out=w4_p[:].rearrange("p a (i q e) -> p a q i e", i=4, e=2),
+                        in_=w4_raw[:].rearrange("p a (q i e) -> p a q i e", i=4, e=2),
+                    )
+            if b == 0:
+                x[0] = wide.tile([P, 4, M], F32, name="x0", tag="wide")
+            else:
+                x[1, 0] = wide.tile([P, 4, 256], F32, name="x10", tag="wide")
             for i in range(4):
-                for s in range(2):
-                    stage1(accs0[i][s], 0, i, s, a)
-            if a == 0:
-                nc.vector.tensor_copy(
-                    out=w4_p[:].rearrange("p a (i q e) -> p a q i e", i=4, e=2),
-                    in_=w4_raw[:].rearrange("p a (q i e) -> p a q i e", i=4, e=2),
-                )
-                nc.vector.tensor_copy(
-                    out=w4s_p[:].rearrange("p a (i q) -> p a q i", i=4),
-                    in_=w4s_raw[:].rearrange("p a (q i) -> p a q i", i=4),
-                )
-        x[0] = wide.tile([P, 4, M], F32, name="x0", tag="wide")
-        for i in range(4):
-            empty_h(0, i, accs0[i])
-            pick(0, i, 0, M)
+                empty_h(b, i, accs[i])
+                pick(b, i, 0, M if b == 0 else 256)
+                if (b, i) == (0, 0):
+                    nc.vector.tensor_copy(
+                        out=w4s_p[:].rearrange("p a (i q) -> p a q i", i=4),
+                        in_=w4s_raw[:].rearrange("p a (q i) -> p a q i", i=4),
+                    )
 
-        x[1, 0] = wide.tile([P, 4, 256], F32, name="x10", tag="wide")
-        nb = 4 if MODE == "T" else 8
-        early = nb // 2
-        accs1 = [[bank((2 * i + s) % nb, "h1_%d%d" % (i, s)) for s in range(2)] for i in range(early)]
-        for a in range(3):
-            quantize_w1(1, a)
-            for i in range(early):
-                for s in range(2):
-                    stage1(accs1[i][s], 1, i, s, a)
+        pages = [held.tile([P, T2], F32, name="page%d" % i, tag="page%d" % i) for i in range(4)]
         for i in range(4):
-            if i >= early:
-                accs1.append([bank((2 * i + s) % nb, "h1_%d%d" % (i, s)) for s in range(2)])
-                for s in range(2):
-                    for a in range(3):
-                        stage1(accs1[i][s], 1, i, s, a)
-            empty_h(1, i, accs1[i])
-            pick(1, i, 0, 256)
-        x[1, 1] = held.tile([P, 4, 256], F32, name="x11", tag="gain_then_x")
-        for i in range(4):
-            pick(1, i, 256, 512)
+            nc.vector.memset(pages[i][:], 0.0)
 
         zc, zs, ysb = {}, {}, {}
 
-        def make_z_T(b, c):
-            cols = slice(128 * c, 128 * (c + 1))
-            turned = bank((2 if b == 1 and c >= 2 else 4) + c % 2, "turned%d%d" % (b, c))
-            for i in range(4):
-                nc.tensor.matmul(
-                    turned[:, 128 * i : 128 * (i + 1)], hum_t[b][:, i, cols], ident[:],
-                    start=(i == 0), stop=False, is_transpose=True,
-                )
-            for i in range(4):
-                nc.tensor.matmul(
-                    turned[:, 128 * i : 128 * (i + 1)], x_at(b, i, 128 * c, 128 * (c + 1)), ident[:],
-                    start=False, stop=(i == 3), is_transpose=True,
-                )
-            bounded = ring.tile([P, 512], F32, name="bounded%d%d" % (b, c), tag="bounded")
-            nc.scalar.activation(out=bounded[:], in_=turned[:], func=ACT.Tanh)
-            back = bank(6 + c % 2, "back%d%d" % (b, c))
-            for i in range(4):
-                nc.tensor.transpose(back[:, 128 * i : 128 * (i + 1)], bounded[:, 128 * i : 128 * (i + 1)], ident[:])
-            zb = held.tile([P, 128, 4], BF16, name="zb%d%d" % (b, c), tag="zb%d" % c, align_bytes=64)
-            nc.vector.tensor_tensor(
-                zb[:], back[:].rearrange("p (i m) -> p m i", i=4), lift_t[:, b : b + 1, :].to_broadcast([P, 128, 4]), MULT
-            )
-            return zb
-
-        def make_z_S(b, c):
-            cols = slice(128 * c, 128 * (c + 1))
-            summed = ring.tile([P, 4, 128], F32, name="summed%d%d" % (b, c), tag="summed")
-            nc.vector.tensor_tensor(summed[:], x_at(b, slice(0, 4), 128 * c, 128 * (c + 1)), hum_t[b][:, :, cols], ADD)
-            bounded = ring.tile([P, 128, 4], F32, name="bounded%d%d" % (b, c), tag="bounded")
-            nc.scalar.activation(out=bounded[:], in_=summed[:].rearrange("p i m -> p m i"), func=ACT.Tanh)
-            zb = held.tile([P, 128, 4], BF16, name="zb%d%d" % (b, c), tag="zb%d" % c, align_bytes=64)
-            nc.vector.tensor_tensor(zb[:], bounded[:], lift_t[:, b : b + 1, :].to_broadcast([P, 128, 4]), MULT)
-            return zb
-
-        def make_z(b, pair):
-            made = [(c, (make_z_T if MODE == "T" else make_z_S)(b, c)) for c in pair]
-            for c, zb in made:
-                zc[b, c] = held.tile([P, 128], U32, name="zc%d%d" % (b, c), align_bytes=64)
-                zs[b, c] = held.tile([P, 128], U8, name="zs%d%d" % (b, c), align_bytes=64)
+        def make_z(b, spans):
+            made = []
+            for lo, hi in spans:
+                n = hi - lo
+                summed = pair.tile([P, 4, n], F32, name="summed%d%d" % (b, lo), tag="summed")
+                nc.vector.tensor_tensor(summed[:], x_at(b, slice(0, 4), lo, hi), hum_t[b][:, :, lo:hi], ADD)
+                bounded = pair.tile([P, n, 4], F32, name="bounded%d%d" % (b, lo), tag="bounded")
+                nc.scalar.activation(out=bounded[:], in_=summed[:].rearrange("p i m -> p m i"), func=ACT.Tanh)
+                made.append((lo, n, bounded))
+            rounded = []
+            for lo, n, bounded in made:
+                zb = held.tile([P, n, 4], BF16, name="zb%d%d" % (b, lo), tag="zb%d" % lo, align_bytes=64)
+                nc.vector.tensor_tensor(zb[:], bounded[:], lift_t[:, b : b + 1, :].to_broadcast([P, n, 4]), MULT)
+                rounded.append((lo, n, zb))
+            for lo, n, zb in rounded:
+                words = held.tile([P, n], U32, name="zc%d%d" % (b, lo), align_bytes=64)
+                plane = held.tile([P, n], U8, name="zs%d%d" % (b, lo), align_bytes=64)
                 nc.vector.quantize_mx(
-                    out=zc[b, c][:].bitcast(FP8X4), scales=zs[b, c][:], in_=zb[:].rearrange("p m i -> p (m i)")
+                    out=words[:].bitcast(FP8X4), scales=plane[:], in_=zb[:].rearrange("p m i -> p (m i)")
                 )
+                for k in range(n // 128):
+                    zc[b, lo // 128 + k] = words[:, 128 * k : 128 * (k + 1)]
+                    zs[b, lo // 128 + k] = plane[:, 128 * k : 128 * (k + 1)]
 
-        make_z(0, (0, 1))
-        make_z(0, (2, 3))
-        make_z(1, (0, 1))
-        ybs = {}
+        def make_z_turned(b, chunks):
+            made = []
+            for c in chunks:
+                turned = bank(c, "turned%d%d" % (b, c))
+                for i in range(4):
+                    nc.tensor.matmul(
+                        turned[:, 128 * i : 128 * (i + 1)], hum_t[b][:, i, 128 * c : 128 * (c + 1)], ident[:],
+                        start=(i == 0), stop=False, is_transpose=True,
+                    )
+                for i in range(4):
+                    nc.tensor.matmul(
+                        turned[:, 128 * i : 128 * (i + 1)], x_at(b, i, 128 * c, 128 * (c + 1)), ident[:],
+                        start=False, stop=(i == 3), is_transpose=True,
+                    )
+                bounded = pair.tile([P, 512], F32, name="bounded%d%d" % (b, c), tag="bounded")
+                nc.scalar.activation(out=bounded[:], in_=turned[:], func=ACT.Tanh)
+                back = bank(4 + c % 2, "back%d%d" % (b, c))
+                for i in range(4):
+                    nc.tensor.transpose(back[:, 128 * i : 128 * (i + 1)], bounded[:, 128 * i : 128 * (i + 1)], ident[:])
+                made.append((c, back))
+            rounded = []
+            for c, back in made:
+                zb = held.tile([P, 128, 4], BF16, name="zb%d%d" % (b, c), tag="zb%d" % (128 * c), align_bytes=64)
+                nc.vector.tensor_tensor(
+                    zb[:], back[:].rearrange("p (i m) -> p m i", i=4), lift_t[:, b : b + 1, :].to_broadcast([P, 128, 4]), MULT
+                )
+                rounded.append((c, zb))
+            for c, zb in rounded:
+                words = held.tile([P, 128], U32, name="zc%d%d" % (b, c), align_bytes=64)
+                plane = held.tile([P, 128], U8, name="zs%d%d" % (b, c), align_bytes=64)
+                nc.vector.quantize_mx(
+                    out=words[:].bitcast(FP8X4), scales=plane[:], in_=zb[:].rearrange("p m i -> p (m i)")
+                )
+                zc[b, c] = words[:]
+                zs[b, c] = plane[:]
+
+        make_z(0, ((0, 256), (256, 512)))
+        make_z_turned(1, (0, 1))
         for hf in range(2):
-            yb = [bank(4 * hf + ip, "y%d%d" % (hf, ip)) for ip in range(2)]
+            yb = [bank(6 * (1 - hf) + ip, "y%d%d" % (hf, ip)) for ip in range(2)]
             for b in range(2):
                 for ip in range(2):
                     parts = [(i, c) for i in (2 * ip, 2 * ip + 1) for c in (2 * hf, 2 * hf + 1)]
@@ -274,16 +294,18 @@ def tile_list_leaf_grade_trays_kernel(
                             out=yb[ip][:, at : at + 128],
                             lhsT=w4_p[:, b, 256 * i : 256 * (i + 1)].bitcast(FP4X4),
                             lhsT_scale=w4s_p[:, b, 128 * i : 128 * (i + 1)],
-                            rhs=zc[b, c][:].bitcast(FP8X4),
-                            rhs_scale=zs[b, c][:],
+                            rhs=zc[b, c].bitcast(FP8X4),
+                            rhs_scale=zs[b, c],
                             start=(b == 0 and (i, c) == parts[0]),
                             stop=(b == 1 and (i, c) == parts[-1]),
                         )
-            ybs[hf] = yb
             if hf == 0:
-                make_z(1, (2, 3))
+                x[1, 1] = held.tile([P, 4, 256], F32, name="x11", tag="gain_then_x")
+                for i in range(4):
+                    pick(1, i, 256, 512)
+                make_z_turned(1, (2, 3))
             for i in range(4):
-                tag = "zb%d" % (i + 1) if (hf == 0 and i in (1, 2)) else "ysb%d%d" % (hf, i)
+                tag = "zb384" if (hf, i) == (0, 1) else "ysb%d%d" % (hf, i)
                 ysb[hf, i] = held.tile([P, 256], F32, name="ysb%d%d" % (hf, i), tag=tag, align_bytes=64)
                 nc.scalar.activation(
                     out=ysb[hf, i][:], in_=yb[i // 2][:, 256 * (i % 2) : 256 * (i % 2) + 256],

@@ -19,7 +19,7 @@ MULT = mybir.AluOpType.mult
 ADD = mybir.AluOpType.add
 
 P = 128
-VECTOR_CASTS = ((0, 2, 0),)
+VECTOR_CASTS = ((0, 2, 0), (1, 1, 0), (1, 2, 0))
 SCALE_QUEUE = "gpsimd"
 
 
@@ -130,7 +130,7 @@ def tile_list_leaf_grade_trays_kernel(
         codes, scales = {}, {}
 
         def quantize_w1(b, a):
-            parts = 2 if a == 2 else 1
+            parts = 2 if (b, a, 0) in VECTOR_CASTS else 1
             wt = 4 // parts
             grouped = []
             for u in range(parts):

from contextlib import ExitStack

import concourse.mybir as mybir
from concourse.masks import make_identity

K, T, H, S, M, N, T2 = 1536, 4096, 1024, 1024, 512, 512, 1024
FLOPS = 2 * K * H * S + 2 * H * N * M

F32 = mybir.dt.float32
BF16 = mybir.dt.bfloat16
I32 = mybir.dt.int32
U32 = mybir.dt.uint32
U16 = mybir.dt.uint16
U8 = mybir.dt.uint8
FP8X4 = mybir.dt.float8_e4m3fn_x4
FP4X4 = mybir.dt.float4_e2m1fn_x4
ACT = mybir.ActivationFunctionType
MULT = mybir.AluOpType.mult
ADD = mybir.AluOpType.add

P = 128
VECTOR_CASTS = ((0, 2, 0), (1, 1, 0), (1, 2, 0))
SCALE_QUEUE = "gpsimd"


def tile_list_leaf_grade_trays_kernel(
    tc, tab_words, tab_scales, offs, w1, gain, offs2, wgt, hum, lift, w4_words, w4_scales, base, offs3, wgo, out
):
    nc = tc.nc
    with ExitStack() as ctx:
        lists = ctx.enter_context(tc.tile_pool(name="lists", bufs=1))
        held = ctx.enter_context(tc.tile_pool(name="held", bufs=1))
        ring = ctx.enter_context(tc.tile_pool(name="ring", bufs=4))
        pair = ctx.enter_context(tc.tile_pool(name="pair", bufs=2))
        wide = ctx.enter_context(tc.tile_pool(name="wide", bufs=6))
        psum = ctx.enter_context(tc.psum_pool(name="psum", bufs=1))

        def bank(n, name):
            return psum.tile([P, 512], F32, name=name, tag="bank%d" % n)

        tab_s = held.tile([P, T], U8, name="tab_s", tag="page1")
        nc.vector.memset(tab_s[:].bitcast(I32), 0)
        w4s_raw = held.tile([P, 2, N], U8, name="w4s_raw")
        nc.vector.memset(w4s_raw[:].bitcast(I32), 0)

        tab_w = [held.tile([P, T], U32, name="tab_w%d" % a, tag=("page0", "page2", "tab_w2")[a]) for a in range(3)]
        raw = {}

        def load_tab(a, pieces=1):
            words = tab_words[a].rearrange("p t i -> p (t i)").bitcast(I32)
            for lo in range(0, T, T // pieces):
                hi = lo + T // pieces
                nc.sync.dma_start(out=tab_w[a][:, lo:hi].bitcast(I32), in_=words[:, lo:hi])

        def load_w1(b, a, pieces=1):
            raw[b, a] = wide.tile([P, 4, 512], F32, name="raw%d%d" % (b, a), tag="wide")
            rows = w1[512 * a : 512 * (a + 1), 512 * b : 512 * (b + 1)].rearrange("(p j) c -> p j c", j=4)
            for lo in range(0, 4, 4 // pieces):
                hi = lo + 4 // pieces
                nc.sync.dma_start(out=raw[b, a][:, lo:hi, :], in_=rows[:, lo:hi, :])

        def load_tab_scales(queue):
            for q in range(4):
                queue.dma_start(
                    out=tab_s[32 * q : 32 * q + 12, :].bitcast(I32), in_=tab_scales[:, 4 * q : 4 * q + 4, :].bitcast(I32)
                )

        def load_w4_scales(queue):
            for q in range(4):
                queue.dma_start(
                    out=w4s_raw[32 * q : 32 * q + 4, :, :].bitcast(I32),
                    in_=w4_scales[:, 4 * q : 4 * q + 4, :].rearrange("a r n -> r a n").bitcast(I32),
                )

        def load_hum(b):
            nc.sync.dma_start(out=hum_t[b][:], in_=hum[512 * b : 512 * (b + 1), :].rearrange("(p i) m -> p i m", i=4))

        list1 = lists.tile([P, S // 16], U16, name="list1")
        list2 = lists.tile([P, M // 16], U16, name="list2")
        list3 = lists.tile([P, M // 16], U16, name="list3")
        gain_t = held.tile([P, 2, 4], F32, name="gain_t", tag="gain_then_x")
        lift_t = held.tile([P, 2, 4], F32, name="lift_t")
        base_t = held.tile([P, 4], F32, name="base_t")
        w4_raw = held.tile([P, 2, 2 * N], U8, name="w4_raw", tag="page3")
        wgt_t = held.tile([P, M], F32, name="wgt_t")
        wgo_t = held.tile([P, M], F32, name="wgo_t")
        hum_t = [held.tile([P, 4, M], F32, name="hum_t%d" % b) for b in range(2)]

        def load_small(which):
            if which == "gain":
                nc.sync.dma_start(out=gain_t[:], in_=gain.rearrange("(b p i) -> p b i", b=2, i=4))
            if which == "lift":
                nc.sync.dma_start(out=lift_t[:], in_=lift.rearrange("(b p i) -> p b i", b=2, i=4))
            if which == "list2":
                nc.sync.dma_start(list2[:], offs2)
            if which == "list3":
                nc.sync.dma_start(list3[:], offs3)

        pieces = 4 if SCALE_QUEUE == "sync" else 1
        load_tab(0, pieces)
        nc.sync.dma_start(list1[:], offs)
        load_w1(0, 0, 2 if SCALE_QUEUE == "sync" else 1)
        nc.sync.dma_start(out=w4_raw[:].bitcast(I32), in_=w4_words.rearrange("a p c -> p a c").bitcast(I32))
        load_tab_scales(nc.sync if SCALE_QUEUE == "sync" else nc.gpsimd)
        load_tab(1)
        load_w1(0, 1)
        load_w4_scales(nc.sync)
        load_tab(2)
        load_w1(0, 2)
        load_small("gain")
        load_small("list2")
        nc.sync.dma_start(out=wgt_t[:], in_=wgt)
        load_w1(1, 0)
        load_w1(1, 1)
        load_hum(0)
        load_w1(1, 2)
        load_small("lift")
        load_hum(1)
        load_small("list3")
        nc.sync.dma_start(out=base_t[:], in_=base.rearrange("(p i) -> p i", i=4))
        nc.sync.dma_start(out=wgo_t[:], in_=wgo)

        ident = held.tile([P, P], F32, name="ident")
        make_identity(nc, ident[:])


        got_w = [held.tile([P, S], U32, name="got_w%d" % a, align_bytes=64) for a in range(3)]
        got_s = held.tile([P, S], U8, name="got_s", align_bytes=64)

        codes, scales = {}, {}

        def quantize_w1(b, a):
            parts = 2 if (b, a, 0) in VECTOR_CASTS else 1
            wt = 4 // parts
            grouped = []
            for u in range(parts):
                g = ring.tile([P, 512 * wt], BF16, name="grouped%d%d%d" % (b, a, u), tag="grouped", align_bytes=64)
                dst = g[:].rearrange("p (t m j) -> p m j t", t=wt, j=4)
                src = raw[b, a][:].rearrange("p j (m t) -> p m j t", t=4)[:, :, :, wt * u : wt * (u + 1)]
                if (b, a, u) in VECTOR_CASTS:
                    nc.vector.tensor_copy(out=dst, in_=src)
                else:
                    nc.scalar.activation(out=dst, in_=src, func=ACT.Copy)
                grouped.append(g)
            for u in range(parts):
                words = held.tile([P, 128 * wt], U32, name="codes%d%d%d" % (b, a, u), align_bytes=64)
                plane = held.tile([P, 128 * wt], U8, name="scales%d%d%d" % (b, a, u), align_bytes=64)
                nc.vector.quantize_mx(out=words[:].bitcast(FP8X4), scales=plane[:], in_=grouped[u][:])
                for t in range(wt):
                    codes[b, a, wt * u + t] = words[:, 128 * t : 128 * (t + 1)]
                    scales[b, a, wt * u + t] = plane[:, 128 * t : 128 * (t + 1)]

        def stage1(acc, b, i, s, a):
            nc.tensor.matmul_mx(
                out=acc[:],
                lhsT=codes[b, a, i].bitcast(FP8X4),
                lhsT_scale=scales[b, a, i],
                rhs=got_w[a][:, 512 * s : 512 * (s + 1)].bitcast(FP8X4),
                rhs_scale=got_s[4 * a : P, 512 * s : 512 * (s + 1)],
                start=(a == 0),
                stop=(a == 2),
            )

        x = {}
        h = {}

        def empty_h(b, i, accs):
            h[b, i] = ring.tile([P, S], F32, name="h%d%d" % (b, i), tag="h")
            for s in range(2):
                if (b, i, s) == (0, 0, 1):
                    nc.vector.tensor_scalar(h[b, i][:, 512:1024], accs[s][:], gain_t[:, b, i : i + 1], None, MULT)
                else:
                    nc.scalar.activation(
                        out=h[b, i][:, 512 * s : 512 * (s + 1)], in_=accs[s][:], func=ACT.Copy, scale=gain_t[:, b, i : i + 1]
                    )

        def x_at(b, i, lo, hi):
            if b == 0:
                return x[0][:, i, lo:hi]
            return x[1, lo // 256][:, i, lo % 256 : lo % 256 + hi - lo]

        def pick(b, i, lo, hi):
            nc.vector.tensor_tensor(
                x_at(b, i, lo, hi), h[b, i][:].indirect(list2[:, lo // 16 : hi // 16]), wgt_t[:, lo:hi], MULT
            )

        w4_p = held.tile([P, 2, 2 * N], U8, name="w4_p", align_bytes=64)
        w4s_p = held.tile([P, 2, N], U8, name="w4s_p", align_bytes=64)
        for b in range(2):
            accs = [[bank(2 * i + s, "h%d_%d%d" % (b, i, s)) for s in range(2)] for i in range(4)]
            for a in range(3):
                if b == 0:
                    nc.vector.tensor_copy(got_w[a][:], tab_w[a][:].indirect(list1[:]))
                    if a == 0:
                        nc.vector.tensor_copy(got_s[:], tab_s[:].indirect(list1[:]))
                quantize_w1(b, a)
                for i in range(4):
                    for s in range(2):
                        stage1(accs[i][s], b, i, s, a)
                if (b, a) == (0, 0):
                    nc.vector.tensor_copy(
                        out=w4_p[:].rearrange("p a (i q e) -> p a q i e", i=4, e=2),
                        in_=w4_raw[:].rearrange("p a (q i e) -> p a q i e", i=4, e=2),
                    )
            if b == 0:
                x[0] = wide.tile([P, 4, M], F32, name="x0", tag="wide")
            else:
                x[1, 0] = wide.tile([P, 4, 256], F32, name="x10", tag="wide")
            for i in range(4):
                empty_h(b, i, accs[i])
                pick(b, i, 0, M if b == 0 else 256)
                if (b, i) == (0, 0):
                    nc.vector.tensor_copy(
                        out=w4s_p[:].rearrange("p a (i q) -> p a q i", i=4),
                        in_=w4s_raw[:].rearrange("p a (q i) -> p a q i", i=4),
                    )

        pages = [held.tile([P, T2], F32, name="page%d" % i, tag="page%d" % i) for i in range(4)]
        for i in range(4):
            nc.vector.memset(pages[i][:], 0.0)

        zc, zs, ysb = {}, {}, {}

        def make_z(b, spans):
            made = []
            for lo, hi in spans:
                n = hi - lo
                summed = pair.tile([P, 4, n], F32, name="summed%d%d" % (b, lo), tag="summed")
                nc.vector.tensor_tensor(summed[:], x_at(b, slice(0, 4), lo, hi), hum_t[b][:, :, lo:hi], ADD)
                bounded = pair.tile([P, n, 4], F32, name="bounded%d%d" % (b, lo), tag="bounded")
                nc.scalar.activation(out=bounded[:], in_=summed[:].rearrange("p i m -> p m i"), func=ACT.Tanh)
                made.append((lo, n, bounded))
            rounded = []
            for lo, n, bounded in made:
                zb = held.tile([P, n, 4], BF16, name="zb%d%d" % (b, lo), tag="zb%d" % lo, align_bytes=64)
                nc.vector.tensor_tensor(zb[:], bounded[:], lift_t[:, b : b + 1, :].to_broadcast([P, n, 4]), MULT)
                rounded.append((lo, n, zb))
            for lo, n, zb in rounded:
                words = held.tile([P, n], U32, name="zc%d%d" % (b, lo), align_bytes=64)
                plane = held.tile([P, n], U8, name="zs%d%d" % (b, lo), align_bytes=64)
                nc.vector.quantize_mx(
                    out=words[:].bitcast(FP8X4), scales=plane[:], in_=zb[:].rearrange("p m i -> p (m i)")
                )
                for k in range(n // 128):
                    zc[b, lo // 128 + k] = words[:, 128 * k : 128 * (k + 1)]
                    zs[b, lo // 128 + k] = plane[:, 128 * k : 128 * (k + 1)]

        def make_z_turned(b, chunks):
            made = []
            for c in chunks:
                turned = bank(c, "turned%d%d" % (b, c))
                for i in range(4):
                    nc.tensor.matmul(
                        turned[:, 128 * i : 128 * (i + 1)], hum_t[b][:, i, 128 * c : 128 * (c + 1)], ident[:],
                        start=(i == 0), stop=False, is_transpose=True,
                    )
                for i in range(4):
                    nc.tensor.matmul(
                        turned[:, 128 * i : 128 * (i + 1)], x_at(b, i, 128 * c, 128 * (c + 1)), ident[:],
                        start=False, stop=(i == 3), is_transpose=True,
                    )
                bounded = pair.tile([P, 512], F32, name="bounded%d%d" % (b, c), tag="bounded")
                nc.scalar.activation(out=bounded[:], in_=turned[:], func=ACT.Tanh)
                back = bank(4 + c % 2, "back%d%d" % (b, c))
                for i in range(4):
                    nc.tensor.transpose(back[:, 128 * i : 128 * (i + 1)], bounded[:, 128 * i : 128 * (i + 1)], ident[:])
                made.append((c, back))
            rounded = []
            for c, back in made:
                zb = held.tile([P, 128, 4], BF16, name="zb%d%d" % (b, c), tag="zb%d" % (128 * c), align_bytes=64)
                nc.vector.tensor_tensor(
                    zb[:], back[:].rearrange("p (i m) -> p m i", i=4), lift_t[:, b : b + 1, :].to_broadcast([P, 128, 4]), MULT
                )
                rounded.append((c, zb))
            for c, zb in rounded:
                words = held.tile([P, 128], U32, name="zc%d%d" % (b, c), align_bytes=64)
                plane = held.tile([P, 128], U8, name="zs%d%d" % (b, c), align_bytes=64)
                nc.vector.quantize_mx(
                    out=words[:].bitcast(FP8X4), scales=plane[:], in_=zb[:].rearrange("p m i -> p (m i)")
                )
                zc[b, c] = words[:]
                zs[b, c] = plane[:]

        make_z(0, ((0, 256), (256, 512)))
        make_z_turned(1, (0, 1))
        for hf in range(2):
            yb = [bank(6 * (1 - hf) + ip, "y%d%d" % (hf, ip)) for ip in range(2)]
            for b in range(2):
                for ip in range(2):
                    parts = [(i, c) for i in (2 * ip, 2 * ip + 1) for c in (2 * hf, 2 * hf + 1)]
                    for i, c in parts:
                        at = 256 * (i % 2) + 128 * (c % 2)
                        nc.tensor.matmul_mx(
                            out=yb[ip][:, at : at + 128],
                            lhsT=w4_p[:, b, 256 * i : 256 * (i + 1)].bitcast(FP4X4),
                            lhsT_scale=w4s_p[:, b, 128 * i : 128 * (i + 1)],
                            rhs=zc[b, c].bitcast(FP8X4),
                            rhs_scale=zs[b, c],
                            start=(b == 0 and (i, c) == parts[0]),
                            stop=(b == 1 and (i, c) == parts[-1]),
                        )
            if hf == 0:
                x[1, 1] = held.tile([P, 4, 256], F32, name="x11", tag="gain_then_x")
                for i in range(4):
                    pick(1, i, 256, 512)
                make_z_turned(1, (2, 3))
            for i in range(4):
                tag = "zb384" if (hf, i) == (0, 1) else "ysb%d%d" % (hf, i)
                ysb[hf, i] = held.tile([P, 256], F32, name="ysb%d%d" % (hf, i), tag=tag, align_bytes=64)
                nc.scalar.activation(
                    out=ysb[hf, i][:], in_=yb[i // 2][:, 256 * (i % 2) : 256 * (i % 2) + 256],
                    func=ACT.Identity, bias=base_t[:, i : i + 1],
                )

        rows = out.rearrange("(p i) t -> p i t", i=4)
        for hf in range(2):
            for i in range(4):
                nc.vector.tensor_tensor(
                    pages[i][:].indirect(list3[:, 16 * hf : 16 * hf + 16]),
                    ysb[hf, i][:], wgo_t[:, 256 * hf : 256 * (hf + 1)], MULT,
                )
                if hf == 1:
                    nc.sync.dma_start(out=rows[:, i, :], in_=pages[i][:])
